import numpy as np
import ml_dtypes


def mxq(x, axis, fmt="e4m3"):
    dtype, down = {"e4m3": (ml_dtypes.float8_e4m3fn, 7), "e5m2": (ml_dtypes.float8_e5m2, 14)}[fmt]
    v = np.moveaxis(np.asarray(x, np.float32).astype(ml_dtypes.bfloat16).astype(np.float64), axis, -1)
    blocks = v.reshape(v.shape[:-1] + (-1, 32))
    amax = np.abs(blocks).max(-1, keepdims=True)
    byte = np.maximum(np.where(amax > 0, np.frexp(amax)[1] - 1 + 127, 0) - down, 1)
    scale = np.exp2(byte - 127.0)
    codes = (blocks / scale).astype(np.float32).astype(dtype).astype(np.float64)
    return np.moveaxis((codes * scale).reshape(v.shape), -1, axis)


WIDE = False


def mx_kscale(k):
    if not WIDE:
        return np.ones(k)
    levels = np.array([10, -10, 5, -5, 0])
    if k % 512:
        return np.exp2(np.random.permutation(np.resize(levels, k // 32))).repeat(32)
    a = np.empty((k // 512, 16))
    for p in range(k // 512):
        a[p, :8] = np.random.permutation(np.resize(levels, 8))
        for g in range(8):
            far = levels[np.abs(levels - a[p, g]) >= 10]
            a[p, g + 8] = far[np.random.randint(len(far))]
    return np.exp2(a.ravel()).repeat(32)


def f64(x):
    return np.asarray(x).astype(np.float64)


def striped(idx):
    return np.tile(np.asarray(idx).reshape(-1, 16).T, (8, 1)).astype(np.uint16)


def unstriped(offs):
    return offs[:16].T.reshape(-1).astype(np.int64)


B, N, T, D, DV, NQ = 1, 512, 2048, 1536, 128, 128


def setup_inputs():
    n = np.random.standard_normal
    idx = np.random.permutation(T)[:B * N]
    s = mx_kscale(D)[:, None]
    u = np.ones(T)
    u[idx] = mx_kscale(B * N)
    r = np.random.uniform(0.5, 2.0, T)
    k = n((D, T)) / s
    v = n((DV, T)) / (u * r)
    return {
        "qT": (n((B, D, NQ)) * s * (0.80 / np.sqrt(D))).astype(np.float32),
        "kT": k.astype(np.float32),
        "vT": v.astype(np.float32),
        "vs": np.tile(u * r, (128, 1)).astype(np.float32),
        "offs": striped(idx),
    }


def reference(qT, kT, vT, vs, offs):
    idx = unstriped(offs)
    k = f64(kT)
    v = f64(vT)
    pick = lambda x: x[:, idx].reshape(x.shape[0], B, N).transpose(1, 0, 2)
    q = f64(qT)
    score = mxq(q, 1, "e4m3").transpose(0, 2, 1) @ mxq(pick(k), 1, "e4m3")
    m = score.max(-1, keepdims=True)
    p = np.exp(score - m)
    total = p.sum(-1, keepdims=True)
    w = p * pick(f64(vs))[:, :1, :]
    y = mxq(w, 2, "e4m3") @ mxq(pick(v).transpose(0, 2, 1), 1, "e4m3")
    y = y / total
    return y

@@ -1,0 +1,232 @@
+from contextlib import ExitStack
+
+import concourse.mybir as mybir
+from concourse.masks import make_identity
+
+P = 128
+D = 1536
+T = 2048
+N = 512
+NQ = 128
+DV = 128
+PACK = 4
+K_PASS = P * PACK
+PASSES = D // K_PASS
+S = N // PACK
+HALF = N // 2
+
+FLOPS = 2 * NQ * N * D + 2 * NQ * N * DV
+BYTES = 4 * (D * T + DV * T + T + D * NQ + NQ * DV) + 2 * P * (N // 16)
+
+F32 = mybir.dt.float32
+BF16 = mybir.dt.bfloat16
+U32 = mybir.dt.uint32
+U16 = mybir.dt.uint16
+U8 = mybir.dt.uint8
+FP8X4 = mybir.dt.float8_e4m3fn_x4
+Exp = mybir.ActivationFunctionType.Exp
+Copy = mybir.ActivationFunctionType.Copy
+mult = mybir.AluOpType.mult
+max_op = mybir.AluOpType.max
+X = mybir.AxisListType.X
+
+
+def tile_attend_knn_kernel(tc, qT, kT, vT, vs, offs, out):
+    nc = tc.nc
+    with ExitStack() as ctx:
+        keep = ctx.enter_context(tc.tile_pool(name="keep", bufs=1))
+        psum = ctx.enter_context(tc.psum_pool(name="psum", bufs=1))
+
+        offsets = keep.tile([P, N // 16], U16, name="offsets")
+        nc.sync.dma_start(offsets[:], offs)
+
+        vs_pool = keep.tile([P, T], F32, name="vs_pool")
+        nc.vector.memset(vs_pool[:], 0.0)
+
+        k_rows = kT.rearrange("(g p j) w -> g p j w", p=P, j=PACK)
+        q_rows = qT.rearrange("b (g p j) w -> b g p j w", p=P, j=PACK)
+        k_pool = []
+        q_raw = []
+
+        def load_k(g, j):
+            tile = keep.tile([P, T], F32, name=f"k_pool_{g}_{j}")
+            nc.sync.dma_start(tile[:], k_rows[g, :, j, :])
+            k_pool.append(tile)
+
+        def load_q(g):
+            tile = keep.tile([P, PACK, NQ], F32, name=f"q_raw_{g}")
+            nc.sync.dma_start(tile[:], q_rows[0, g])
+            q_raw.append(tile)
+
+        for g in range(PASSES):
+            for j in range(PACK):
+                if g == 2 and j == 3:
+                    load_q(0)
+                load_k(g, j)
+                if g == 0 and j == 0:
+                    nc.sync.dma_start(vs_pool[0:1, :], vs[0:1, :])
+        load_q(1)
+        load_q(2)
+        v_pool = keep.tile([P, T], F32, name="v_pool")
+        nc.sync.dma_start(v_pool[:], vT)
+
+        ident_f32 = keep.tile([P, P], F32, name="ident_f32")
+        make_identity(nc, ident_f32[:])
+        ident_bf16 = keep.tile([P, P], BF16, name="ident_bf16")
+        make_identity(nc, ident_bf16[:])
+        warm = keep.tile([P, 1], F32, name="warm")
+        nc.scalar.activation(warm[:], ident_f32[:, 0:1], Exp)
+
+        score = [psum.tile([P, HALF], F32, name=f"score_{h}") for h in range(2)]
+        k_grouped = []
+        k_codes = []
+        k_scales = []
+        q_grouped = []
+        q_codes = []
+        q_scales = []
+        for g in range(PASSES):
+            k_grouped.append(keep.tile([P, PACK, S, PACK], BF16, name=f"k_grouped_{g}", align_bytes=64))
+            k_codes.append(keep.tile([P, N], U32, name=f"k_codes_{g}", align_bytes=64))
+            k_scales.append(keep.tile([P, N], U8, name=f"k_scales_{g}", align_bytes=64))
+            q_grouped.append(keep.tile([P, NQ, PACK], BF16, name=f"q_grouped_{g}", align_bytes=64))
+            q_codes.append(keep.tile([P, NQ], U32, name=f"q_codes_{g}", align_bytes=64))
+            q_scales.append(keep.tile([P, NQ], U8, name=f"q_scales_{g}", align_bytes=64))
+
+        def gather_k(g, j):
+            nc.vector.tensor_copy(
+                k_grouped[g][:, :, :, j].rearrange("p t s -> p s t"),
+                k_pool[g * PACK + j][:].indirect(offsets[:]),
+            )
+
+        def quantize_k(g, lo, hi):
+            nc.vector.quantize_mx(
+                out=k_codes[g][:, lo:hi].bitcast(FP8X4),
+                scales=k_scales[g][:, lo:hi],
+                in_=k_grouped[g][:].rearrange("p t s j -> p (t s j)")[:, lo * PACK : hi * PACK],
+            )
+
+        def group_q(g):
+            nc.scalar.copy(q_grouped[g][:], q_raw[g][:].rearrange("p j q -> p q j"))
+
+        def quantize_q(g):
+            nc.vector.quantize_mx(
+                out=q_codes[g][:].bitcast(FP8X4),
+                scales=q_scales[g][:],
+                in_=q_grouped[g][:].rearrange("p q j -> p (q j)"),
+            )
+
+        def multiply(g, h):
+            cols = slice(h * HALF, (h + 1) * HALF)
+            nc.tensor.matmul_mx(
+                out=score[h][:],
+                lhsT=q_codes[g][:].bitcast(FP8X4),
+                lhsT_scale=q_scales[g][:],
+                rhs=k_codes[g][:, cols].bitcast(FP8X4),
+                rhs_scale=k_scales[g][:, cols],
+                start=(g == 0),
+                stop=(g == PASSES - 1),
+            )
+
+        for g in range(PASSES - 1):
+            for j in range(PACK):
+                gather_k(g, j)
+            quantize_k(g, 0, N)
+
+        vs_row = keep.tile([P, N], F32, name="vs_row")
+        nc.vector.tensor_copy(vs_row[:], vs_pool[:].indirect(offsets[:]))
+        vs_turned = psum.tile([P, PACK, P], F32, name="vs_turned")
+        for t in range(PACK):
+            nc.tensor.transpose(vs_turned[:, t, :], vs_row[:, t:N:PACK], ident_f32[:])
+        vs_slot = keep.tile([P, PACK], F32, name="vs_slot")
+        nc.vector.tensor_copy(vs_slot[:], vs_turned[:, :, 0])
+
+        for j in range(PACK - 1):
+            gather_k(2, j)
+        group_q(0)
+        quantize_q(0)
+        multiply(0, 0)
+        multiply(0, 1)
+        gather_k(2, 3)
+        group_q(1)
+        quantize_q(1)
+        multiply(1, 0)
+        multiply(1, 1)
+        group_q(2)
+        quantize_q(2)
+        quantize_k(2, 0, HALF)
+        quantize_k(2, HALF, N)
+        multiply(2, 0)
+        multiply(2, 1)
+
+        m_half = keep.tile([P, 2], F32, name="m_half")
+        neg_m = keep.tile([P, 1], F32, name="neg_m")
+        l_half = keep.tile([P, 2], F32, name="l_half")
+        l_sum = keep.tile([P, 1], F32, name="l_sum")
+        l_inv = keep.tile([P, 1], F32, name="l_inv")
+        prob = keep.tile([P, PACK, S], F32, name="prob")
+        for h in range(2):
+            nc.vector.reduce_max(m_half[:, h : h + 1], score[h][:], axis=X)
+        nc.vector.tensor_scalar(neg_m[:], m_half[:, 0:1], m_half[:, 1:2], -1.0, max_op, mult)
+        for h in range(2):
+            nc.scalar.activation(
+                prob[:, 2 * h : 2 * h + 2, :].rearrange("p t s -> p (t s)"),
+                score[h][:],
+                Exp,
+                bias=neg_m[:],
+                accum_out=l_half[:, h : h + 1],
+            )
+
+        v_slots = keep.tile([P, PACK, S], BF16, name="v_slots")
+        nc.vector.tensor_copy(v_slots[:].rearrange("p t s -> p s t"), v_pool[:].indirect(offsets[:]))
+
+        p_turned = psum.tile([P, PACK, NQ], F32, name="p_turned")
+        for t in range(PACK):
+            nc.tensor.transpose(p_turned[:, t, :], prob[:, t, :], ident_f32[:])
+        v_turned = psum.tile([P, PACK, DV], BF16, name="v_turned")
+        for t in range(PACK):
+            nc.tensor.transpose(v_turned[:, t, :], v_slots[:, t, :], ident_bf16[:])
+
+        w_grouped = keep.tile([P, NQ, PACK], BF16, name="w_grouped", align_bytes=64)
+        w_codes = keep.tile([P, NQ], U32, name="w_codes", align_bytes=64)
+        w_scales = keep.tile([P, NQ], U8, name="w_scales", align_bytes=64)
+        QH = NQ // 2
+        for h in range(2):
+            qs = slice(h * QH, (h + 1) * QH)
+            nc.vector.tensor_tensor(
+                w_grouped[:, qs, :],
+                p_turned[:, :, qs].rearrange("p t q -> p q t"),
+                vs_slot[:].unsqueeze(1).to_broadcast([P, QH, PACK]),
+                mult,
+            )
+        for h in range(2):
+            qs = slice(h * QH, (h + 1) * QH)
+            nc.vector.quantize_mx(
+                out=w_codes[:, qs].bitcast(FP8X4),
+                scales=w_scales[:, qs],
+                in_=w_grouped[:, qs, :].rearrange("p q t -> p (q t)"),
+            )
+        v_grouped = keep.tile([P, DV, PACK], BF16, name="v_grouped", align_bytes=64)
+        v_codes = keep.tile([P, DV], U32, name="v_codes", align_bytes=64)
+        v_scales = keep.tile([P, DV], U8, name="v_scales", align_bytes=64)
+        nc.scalar.copy(v_grouped[:], v_turned[:].rearrange("p t e -> p e t"))
+        nc.vector.quantize_mx(
+            out=v_codes[:].bitcast(FP8X4),
+            scales=v_scales[:],
+            in_=v_grouped[:].rearrange("p e t -> p (e t)"),
+        )
+        nc.vector.tensor_add(l_sum[:], l_half[:, 0:1], l_half[:, 1:2])
+        nc.vector.reciprocal(l_inv[:], l_sum[:])
+
+        y = psum.tile([P, DV], F32, name="y")
+        nc.tensor.matmul_mx(
+            out=y[:],
+            lhsT=w_codes[:].bitcast(FP8X4),
+            lhsT_scale=w_scales[:],
+            rhs=v_codes[:].bitcast(FP8X4),
+            rhs_scale=v_scales[:],
+            start=True,
+            stop=True,
+        )
+        result = keep.tile([P, DV], F32, name="result")
+        nc.scalar.activation(result[:], y[:], Copy, scale=l_inv[:])
+        nc.sync.dma_start(out[0], result[:])

@@ -27,7 +27,6 @@ FP8X4 = mybir.dt.float8_e4m3fn_x4
 Exp = mybir.ActivationFunctionType.Exp
 Copy = mybir.ActivationFunctionType.Copy
 mult = mybir.AluOpType.mult
-max_op = mybir.AluOpType.max
 X = mybir.AxisListType.X
 
 
@@ -60,13 +59,11 @@ def tile_attend_knn_kernel(tc, qT, kT, vT, vs, offs, out):
 
         for g in range(PASSES):
             for j in range(PACK):
-                if g == 2 and j == 3:
-                    load_q(0)
                 load_k(g, j)
                 if g == 0 and j == 0:
                     nc.sync.dma_start(vs_pool[0:1, :], vs[0:1, :])
-        load_q(1)
-        load_q(2)
+        for g in range(PASSES):
+            load_q(g)
         v_pool = keep.tile([P, T], F32, name="v_pool")
         nc.sync.dma_start(v_pool[:], vT)
 
@@ -77,7 +74,8 @@ def tile_attend_knn_kernel(tc, qT, kT, vT, vs, offs, out):
         warm = keep.tile([P, 1], F32, name="warm")
         nc.scalar.activation(warm[:], ident_f32[:, 0:1], Exp)
 
-        score = [psum.tile([P, HALF], F32, name=f"score_{h}") for h in range(2)]
+        score = psum.tile([P, N], F32, name="score")
+        k_wide = [keep.tile([P, PACK, N], F32, name=f"k_wide_{g}") for g in range(PASSES - 1)]
         k_grouped = []
         k_codes = []
         k_scales = []
@@ -85,24 +83,30 @@ def tile_attend_knn_kernel(tc, qT, kT, vT, vs, offs, out):
         q_codes = []
         q_scales = []
         for g in range(PASSES):
-            k_grouped.append(keep.tile([P, PACK, S, PACK], BF16, name=f"k_grouped_{g}", align_bytes=64))
+            k_grouped.append(keep.tile([P, N, PACK], BF16, name=f"k_grouped_{g}", align_bytes=64))
             k_codes.append(keep.tile([P, N], U32, name=f"k_codes_{g}", align_bytes=64))
             k_scales.append(keep.tile([P, N], U8, name=f"k_scales_{g}", align_bytes=64))
             q_grouped.append(keep.tile([P, NQ, PACK], BF16, name=f"q_grouped_{g}", align_bytes=64))
             q_codes.append(keep.tile([P, NQ], U32, name=f"q_codes_{g}", align_bytes=64))
             q_scales.append(keep.tile([P, NQ], U8, name=f"q_scales_{g}", align_bytes=64))
 
-        def gather_k(g, j):
+        def gather_wide(g, j):
+            nc.vector.tensor_copy(k_wide[g][:, j, :], k_pool[g * PACK + j][:].indirect(offsets[:]))
+
+        def group_k(g):
+            nc.scalar.copy(k_grouped[g][:], k_wide[g][:].rearrange("p j i -> p i j"))
+
+        def gather_k(g, j, lo, hi):
             nc.vector.tensor_copy(
-                k_grouped[g][:, :, :, j].rearrange("p t s -> p s t"),
-                k_pool[g * PACK + j][:].indirect(offsets[:]),
+                k_grouped[g][:, lo:hi, j],
+                k_pool[g * PACK + j][:].indirect(offsets[:, lo // 16 : hi // 16]),
             )
 
         def quantize_k(g, lo, hi):
             nc.vector.quantize_mx(
                 out=k_codes[g][:, lo:hi].bitcast(FP8X4),
                 scales=k_scales[g][:, lo:hi],
-                in_=k_grouped[g][:].rearrange("p t s j -> p (t s j)")[:, lo * PACK : hi * PACK],
+                in_=k_grouped[g][:, lo:hi, :].rearrange("p i j -> p (i j)"),
             )
 
         def group_q(g):
@@ -115,21 +119,21 @@ def tile_attend_knn_kernel(tc, qT, kT, vT, vs, offs, out):
                 in_=q_grouped[g][:].rearrange("p q j -> p (q j)"),
             )
 
-        def multiply(g, h):
-            cols = slice(h * HALF, (h + 1) * HALF)
+        def multiply(g):
             nc.tensor.matmul_mx(
-                out=score[h][:],
+                out=score[:],
                 lhsT=q_codes[g][:].bitcast(FP8X4),
                 lhsT_scale=q_scales[g][:],
-                rhs=k_codes[g][:, cols].bitcast(FP8X4),
-                rhs_scale=k_scales[g][:, cols],
+                rhs=k_codes[g][:].bitcast(FP8X4),
+                rhs_scale=k_scales[g][:],
                 start=(g == 0),
                 stop=(g == PASSES - 1),
             )
 
         for g in range(PASSES - 1):
             for j in range(PACK):
-                gather_k(g, j)
+                gather_wide(g, j)
+            group_k(g)
             quantize_k(g, 0, N)
 
         vs_row = keep.tile([P, N], F32, name="vs_row")
@@ -141,36 +145,31 @@ def tile_attend_knn_kernel(tc, qT, kT, vT, vs, offs, out):
         nc.vector.tensor_copy(vs_slot[:], vs_turned[:, :, 0])
 
         for j in range(PACK - 1):
-            gather_k(2, j)
+            gather_k(2, j, 0, N)
+        gather_k(2, 3, 0, HALF)
+        gather_k(2, 3, HALF, N)
         group_q(0)
         quantize_q(0)
-        multiply(0, 0)
-        multiply(0, 1)
-        gather_k(2, 3)
-        group_q(1)
-        quantize_q(1)
-        multiply(1, 0)
-        multiply(1, 1)
-        group_q(2)
-        quantize_q(2)
+        multiply(0)
         quantize_k(2, 0, HALF)
         quantize_k(2, HALF, N)
-        multiply(2, 0)
-        multiply(2, 1)
+        group_q(1)
+        quantize_q(1)
+        multiply(1)
+        nc.vector.tensor_copy(q_grouped[2][:], q_raw[2][:].rearrange("p j q -> p q j"))
+        quantize_q(2)
+        multiply(2)
 
-        m_half = keep.tile([P, 2], F32, name="m_half")
         neg_m = keep.tile([P, 1], F32, name="neg_m")
         l_half = keep.tile([P, 2], F32, name="l_half")
         l_sum = keep.tile([P, 1], F32, name="l_sum")
         l_inv = keep.tile([P, 1], F32, name="l_inv")
         prob = keep.tile([P, PACK, S], F32, name="prob")
-        for h in range(2):
-            nc.vector.reduce_max(m_half[:, h : h + 1], score[h][:], axis=X)
-        nc.vector.tensor_scalar(neg_m[:], m_half[:, 0:1], m_half[:, 1:2], -1.0, max_op, mult)
+        nc.vector.reduce_max(neg_m[:], score[:], axis=X, negate=True)
         for h in range(2):
             nc.scalar.activation(
-                prob[:, 2 * h : 2 * h + 2, :].rearrange("p t s -> p (t s)"),
-                score[h][:],
+                prob[:, 2 * h : 2 * h + 2, :],
+                score[:].rearrange("p (s t) -> p t s", t=PACK)[:, 2 * h : 2 * h + 2, :],
                 Exp,
                 bias=neg_m[:],
                 accum_out=l_half[:, h : h + 1],

from contextlib import ExitStack

import concourse.mybir as mybir
from concourse.masks import make_identity

P = 128
D = 1536
T = 2048
N = 512
NQ = 128
DV = 128
PACK = 4
K_PASS = P * PACK
PASSES = D // K_PASS
S = N // PACK
HALF = N // 2

FLOPS = 2 * NQ * N * D + 2 * NQ * N * DV
BYTES = 4 * (D * T + DV * T + T + D * NQ + NQ * DV) + 2 * P * (N // 16)

F32 = mybir.dt.float32
BF16 = mybir.dt.bfloat16
U32 = mybir.dt.uint32
U16 = mybir.dt.uint16
U8 = mybir.dt.uint8
FP8X4 = mybir.dt.float8_e4m3fn_x4
Exp = mybir.ActivationFunctionType.Exp
Copy = mybir.ActivationFunctionType.Copy
mult = mybir.AluOpType.mult
X = mybir.AxisListType.X


def tile_attend_knn_kernel(tc, qT, kT, vT, vs, offs, out):
    nc = tc.nc
    with ExitStack() as ctx:
        keep = ctx.enter_context(tc.tile_pool(name="keep", bufs=1))
        psum = ctx.enter_context(tc.psum_pool(name="psum", bufs=1))

        offsets = keep.tile([P, N // 16], U16, name="offsets")
        nc.sync.dma_start(offsets[:], offs)

        vs_pool = keep.tile([P, T], F32, name="vs_pool")
        nc.vector.memset(vs_pool[:], 0.0)

        k_rows = kT.rearrange("(g p j) w -> g p j w", p=P, j=PACK)
        q_rows = qT.rearrange("b (g p j) w -> b g p j w", p=P, j=PACK)
        k_pool = []
        q_raw = []

        def load_k(g, j):
            tile = keep.tile([P, T], F32, name=f"k_pool_{g}_{j}")
            nc.sync.dma_start(tile[:], k_rows[g, :, j, :])
            k_pool.append(tile)

        def load_q(g):
            tile = keep.tile([P, PACK, NQ], F32, name=f"q_raw_{g}")
            nc.sync.dma_start(tile[:], q_rows[0, g])
            q_raw.append(tile)

        for g in range(PASSES):
            for j in range(PACK):
                load_k(g, j)
                if g == 0 and j == 0:
                    nc.sync.dma_start(vs_pool[0:1, :], vs[0:1, :])
        for g in range(PASSES):
            load_q(g)
        v_pool = keep.tile([P, T], F32, name="v_pool")
        nc.sync.dma_start(v_pool[:], vT)

        ident_f32 = keep.tile([P, P], F32, name="ident_f32")
        make_identity(nc, ident_f32[:])
        ident_bf16 = keep.tile([P, P], BF16, name="ident_bf16")
        make_identity(nc, ident_bf16[:])
        warm = keep.tile([P, 1], F32, name="warm")
        nc.scalar.activation(warm[:], ident_f32[:, 0:1], Exp)

        score = psum.tile([P, N], F32, name="score")
        k_wide = [keep.tile([P, PACK, N], F32, name=f"k_wide_{g}") for g in range(PASSES - 1)]
        k_grouped = []
        k_codes = []
        k_scales = []
        q_grouped = []
        q_codes = []
        q_scales = []
        for g in range(PASSES):
            k_grouped.append(keep.tile([P, N, PACK], BF16, name=f"k_grouped_{g}", align_bytes=64))
            k_codes.append(keep.tile([P, N], U32, name=f"k_codes_{g}", align_bytes=64))
            k_scales.append(keep.tile([P, N], U8, name=f"k_scales_{g}", align_bytes=64))
            q_grouped.append(keep.tile([P, NQ, PACK], BF16, name=f"q_grouped_{g}", align_bytes=64))
            q_codes.append(keep.tile([P, NQ], U32, name=f"q_codes_{g}", align_bytes=64))
            q_scales.append(keep.tile([P, NQ], U8, name=f"q_scales_{g}", align_bytes=64))

        def gather_wide(g, j):
            nc.vector.tensor_copy(k_wide[g][:, j, :], k_pool[g * PACK + j][:].indirect(offsets[:]))

        def group_k(g):
            nc.scalar.copy(k_grouped[g][:], k_wide[g][:].rearrange("p j i -> p i j"))

        def gather_k(g, j, lo, hi):
            nc.vector.tensor_copy(
                k_grouped[g][:, lo:hi, j],
                k_pool[g * PACK + j][:].indirect(offsets[:, lo // 16 : hi // 16]),
            )

        def quantize_k(g, lo, hi):
            nc.vector.quantize_mx(
                out=k_codes[g][:, lo:hi].bitcast(FP8X4),
                scales=k_scales[g][:, lo:hi],
                in_=k_grouped[g][:, lo:hi, :].rearrange("p i j -> p (i j)"),
            )

        def group_q(g):
            nc.scalar.copy(q_grouped[g][:], q_raw[g][:].rearrange("p j q -> p q j"))

        def quantize_q(g):
            nc.vector.quantize_mx(
                out=q_codes[g][:].bitcast(FP8X4),
                scales=q_scales[g][:],
                in_=q_grouped[g][:].rearrange("p q j -> p (q j)"),
            )

        def multiply(g):
            nc.tensor.matmul_mx(
                out=score[:],
                lhsT=q_codes[g][:].bitcast(FP8X4),
                lhsT_scale=q_scales[g][:],
                rhs=k_codes[g][:].bitcast(FP8X4),
                rhs_scale=k_scales[g][:],
                start=(g == 0),
                stop=(g == PASSES - 1),
            )

        for g in range(PASSES - 1):
            for j in range(PACK):
                gather_wide(g, j)
            group_k(g)
            quantize_k(g, 0, N)

        vs_row = keep.tile([P, N], F32, name="vs_row")
        nc.vector.tensor_copy(vs_row[:], vs_pool[:].indirect(offsets[:]))
        vs_turned = psum.tile([P, PACK, P], F32, name="vs_turned")
        for t in range(PACK):
            nc.tensor.transpose(vs_turned[:, t, :], vs_row[:, t:N:PACK], ident_f32[:])
        vs_slot = keep.tile([P, PACK], F32, name="vs_slot")
        nc.vector.tensor_copy(vs_slot[:], vs_turned[:, :, 0])

        for j in range(PACK - 1):
            gather_k(2, j, 0, N)
        gather_k(2, 3, 0, HALF)
        gather_k(2, 3, HALF, N)
        group_q(0)
        quantize_q(0)
        multiply(0)
        quantize_k(2, 0, HALF)
        quantize_k(2, HALF, N)
        group_q(1)
        quantize_q(1)
        multiply(1)
        nc.vector.tensor_copy(q_grouped[2][:], q_raw[2][:].rearrange("p j q -> p q j"))
        quantize_q(2)
        multiply(2)

        neg_m = keep.tile([P, 1], F32, name="neg_m")
        l_half = keep.tile([P, 2], F32, name="l_half")
        l_sum = keep.tile([P, 1], F32, name="l_sum")
        l_inv = keep.tile([P, 1], F32, name="l_inv")
        prob = keep.tile([P, PACK, S], F32, name="prob")
        nc.vector.reduce_max(neg_m[:], score[:], axis=X, negate=True)
        for h in range(2):
            nc.scalar.activation(
                prob[:, 2 * h : 2 * h + 2, :],
                score[:].rearrange("p (s t) -> p t s", t=PACK)[:, 2 * h : 2 * h + 2, :],
                Exp,
                bias=neg_m[:],
                accum_out=l_half[:, h : h + 1],
            )

        v_slots = keep.tile([P, PACK, S], BF16, name="v_slots")
        nc.vector.tensor_copy(v_slots[:].rearrange("p t s -> p s t"), v_pool[:].indirect(offsets[:]))

        p_turned = psum.tile([P, PACK, NQ], F32, name="p_turned")
        for t in range(PACK):
            nc.tensor.transpose(p_turned[:, t, :], prob[:, t, :], ident_f32[:])
        v_turned = psum.tile([P, PACK, DV], BF16, name="v_turned")
        for t in range(PACK):
            nc.tensor.transpose(v_turned[:, t, :], v_slots[:, t, :], ident_bf16[:])

        w_grouped = keep.tile([P, NQ, PACK], BF16, name="w_grouped", align_bytes=64)
        w_codes = keep.tile([P, NQ], U32, name="w_codes", align_bytes=64)
        w_scales = keep.tile([P, NQ], U8, name="w_scales", align_bytes=64)
        QH = NQ // 2
        for h in range(2):
            qs = slice(h * QH, (h + 1) * QH)
            nc.vector.tensor_tensor(
                w_grouped[:, qs, :],
                p_turned[:, :, qs].rearrange("p t q -> p q t"),
                vs_slot[:].unsqueeze(1).to_broadcast([P, QH, PACK]),
                mult,
            )
        for h in range(2):
            qs = slice(h * QH, (h + 1) * QH)
            nc.vector.quantize_mx(
                out=w_codes[:, qs].bitcast(FP8X4),
                scales=w_scales[:, qs],
                in_=w_grouped[:, qs, :].rearrange("p q t -> p (q t)"),
            )
        v_grouped = keep.tile([P, DV, PACK], BF16, name="v_grouped", align_bytes=64)
        v_codes = keep.tile([P, DV], U32, name="v_codes", align_bytes=64)
        v_scales = keep.tile([P, DV], U8, name="v_scales", align_bytes=64)
        nc.scalar.copy(v_grouped[:], v_turned[:].rearrange("p t e -> p e t"))
        nc.vector.quantize_mx(
            out=v_codes[:].bitcast(FP8X4),
            scales=v_scales[:],
            in_=v_grouped[:].rearrange("p e t -> p (e t)"),
        )
        nc.vector.tensor_add(l_sum[:], l_half[:, 0:1], l_half[:, 1:2])
        nc.vector.reciprocal(l_inv[:], l_sum[:])

        y = psum.tile([P, DV], F32, name="y")
        nc.tensor.matmul_mx(
            out=y[:],
            lhsT=w_codes[:].bitcast(FP8X4),
            lhsT_scale=w_scales[:],
            rhs=v_codes[:].bitcast(FP8X4),
            rhs_scale=v_scales[:],
            start=True,
            stop=True,
        )
        result = keep.tile([P, DV], F32, name="result")
        nc.scalar.activation(result[:], y[:], Copy, scale=l_inv[:])
        nc.sync.dma_start(out[0], result[:])
